import numpy as np
import ml_dtypes


def mxq(x, axis, fmt="e4m3"):
    dtype, down = {"e4m3": (ml_dtypes.float8_e4m3fn, 7), "e5m2": (ml_dtypes.float8_e5m2, 14)}[fmt]
    v = np.moveaxis(np.asarray(x, np.float32).astype(ml_dtypes.bfloat16).astype(np.float64), axis, -1)
    blocks = v.reshape(v.shape[:-1] + (-1, 32))
    amax = np.abs(blocks).max(-1, keepdims=True)
    byte = np.maximum(np.where(amax > 0, np.frexp(amax)[1] - 1 + 127, 0) - down, 1)
    scale = np.exp2(byte - 127.0)
    codes = (blocks / scale).astype(np.float32).astype(dtype).astype(np.float64)
    return np.moveaxis((codes * scale).reshape(v.shape), -1, axis)


WIDE = False


def mx_kscale(k):
    if not WIDE:
        return np.ones(k)
    levels = np.array([10, -10, 5, -5, 0])
    if k % 512:
        return np.exp2(np.random.permutation(np.resize(levels, k // 32))).repeat(32)
    a = np.empty((k // 512, 16))
    for p in range(k // 512):
        a[p, :8] = np.random.permutation(np.resize(levels, 8))
        for g in range(8):
            far = levels[np.abs(levels - a[p, g]) >= 10]
            a[p, g + 8] = far[np.random.randint(len(far))]
    return np.exp2(a.ravel()).repeat(32)


def f64(x):
    return np.asarray(x).astype(np.float64)


def striped(idx):
    return np.tile(idx.reshape(-1, 16).T, (8, 1)).astype(np.uint16)


def unstriped(offs):
    return offs[:16].T.reshape(-1).astype(np.int64)


E2M1 = np.array([0.0, 0.5, 1.0, 1.5, 2.0, 3.0, 4.0, 6.0, -0.0, -0.5, -1.0, -1.5, -2.0, -3.0, -4.0, -6.0])


def pack_weight(w, fmt):
    k, n = w.shape
    w = f64(np.asarray(w, np.float32).astype(ml_dtypes.bfloat16)).reshape(k // 32, 32, n)
    amax = np.abs(w).max(1)
    if fmt == "e4m3":
        byte = np.frexp(amax)[1] - 1 + 127 - 7
    else:
        mant, ex = np.frexp(amax / 6.0)
        byte = np.where(mant > 0.5, ex, ex - 1) + 127
    byte = np.clip(np.where(amax > 0, byte, 1), 1, 254)
    scaled = (w * np.exp2(127.0 - byte)[:, None, :]).reshape(k, n).astype(np.float32)
    by_word = np.ascontiguousarray(scaled.reshape(k // 512, 128, 4, n).transpose(0, 1, 3, 2))
    if fmt == "e4m3":
        words = by_word.astype(ml_dtypes.float8_e4m3fn).view(np.uint8)
    else:
        c = by_word.astype(ml_dtypes.float4_e2m1fn).view(np.uint8) & 0xF
        words = (c[..., 0::2] | (c[..., 1::2] << 4)).reshape(k // 512, 128, 2 * n)
    return np.ascontiguousarray(words), np.ascontiguousarray(byte.astype(np.uint8).reshape(k // 512, 16, n))


def unpack_weight(words, scales, fmt):
    g, _, n = scales.shape
    words = np.ascontiguousarray(words).reshape(g, 128, n, -1)
    if fmt == "e4m3":
        vals = words.view(ml_dtypes.float8_e4m3fn).astype(np.float64)
    else:
        nib = np.empty((g, 128, n, 4), np.uint8)
        nib[..., 0::2] = words & 0xF
        nib[..., 1::2] = words >> 4
        vals = E2M1[nib]
    vals = vals * np.repeat(np.exp2(scales.astype(np.float64) - 127.0), 8, axis=1)[..., None]
    return vals.transpose(0, 1, 3, 2).reshape(g * 512, n)


def gelu(v):
    return 0.5 * v * (1.0 + np.tanh(np.sqrt(2.0 / np.pi) * (v + 0.044715 * v**3)))


K, K1, K2, H, T, S, T3, S2, P = 1536, 1024, 512, 1024, 4096, 1024, 2048, 1024, 512

def setup_inputs():
    n = np.random.standard_normal
    s = mx_kscale(K)[:, None]
    u = mx_kscale(H)[:, None]
    tab_words, tab_scales = pack_weight(n((K, T)) * s, "e4m3")
    tab2_words, tab2_scales = pack_weight(n((H, T3)) / np.sqrt(H) / u, "e4m3")
    w4_words, w4_scales = pack_weight(1.4 * n((K1, H)) / np.sqrt(K) / s[:K1], "e2m1")
    w1 = 1.4 * n((K2, H)) / np.sqrt(K) / s[K1:]
    return {
        "tab_words": tab_words, "tab_scales": tab_scales,
        "offs": striped(np.random.permutation(T)[:S]),
        "w4_words": w4_words, "w4_scales": w4_scales,
        "w1": w1.astype(np.float32),
        "gain": (np.exp(0.3 * n(H)) * u[:, 0]).astype(np.float32),
        "wish": (0.5 * n((H, S)) * u).astype(np.float32),
        "tab2_words": tab2_words, "tab2_scales": tab2_scales,
        "offs2": striped(np.random.permutation(T3)[:S2]),
        "pos1": striped(np.random.permutation(S)[:P]),
        "pos2": striped(np.random.permutation(S)[:P]),
        "festive": (0.5 * n(S2)).astype(np.float32),
        "favour": np.exp(0.4 * n(S2)).astype(np.float32),
    }

def reference(tab_words, tab_scales, offs, w4_words, w4_scales, w1, gain, wish,
              tab2_words, tab2_scales, offs2, pos1, pos2, festive, favour):
    v = unpack_weight(tab_words, tab_scales, "e4m3")[:, unstriped(offs)]
    v2 = unpack_weight(tab2_words, tab2_scales, "e4m3")[:, unstriped(offs2)]
    w4 = unpack_weight(w4_words, w4_scales, "e2m1")
    wq = mxq(f64(w1), 0, "e4m3")
    d = w4.T @ v[:K1] + wq.T @ v[K1:]
    h = np.tanh(d) * f64(gain)[:, None] + f64(wish)
    x1 = mxq(h[:, unstriped(pos1)], 0, "e4m3")
    x2 = mxq(np.abs(h[:, unstriped(pos2)]), 0, "e4m3")
    e1 = v2.T @ x1
    e2 = v2.T @ x2
    return np.maximum(e1 + f64(festive)[:, None], e2) * f64(favour)[:, None]

@@ -1,0 +1,310 @@
+from contextlib import ExitStack
+
+import concourse.mybir as mybir
+
+F32 = mybir.dt.float32
+BF16 = mybir.dt.bfloat16
+I32 = mybir.dt.int32
+U32 = mybir.dt.uint32
+U16 = mybir.dt.uint16
+U8 = mybir.dt.uint8
+FP8X4 = mybir.dt.float8_e4m3fn_x4
+FP4X4 = mybir.dt.float4_e2m1fn_x4
+ACT = mybir.ActivationFunctionType
+ALU = mybir.AluOpType
+
+P = 128
+PACK = 4
+T, T3 = 4096, 2048
+H, S, S2, NP = 1024, 1024, 1024, 512
+BANK = 512
+QUADS = 4
+M_TILES = S2 // P
+CHUNKS = (256, 128, 128)
+
+FLOPS = 2 * 1536 * H * S + 2 * 2 * H * S2 * NP
+
+
+def tile_list_present_shortlist_scores_kernel(
+    tc, tab_words, tab_scales, offs, w4_words, w4_scales, w1, gain, wish,
+    tab2_words, tab2_scales, offs2, pos1, pos2, festive, favour, out,
+):
+    nc = tc.nc
+    with ExitStack() as ctx:
+        lists = ctx.enter_context(tc.tile_pool(name="lists", bufs=1))
+        keep = ctx.enter_context(tc.tile_pool(name="keep", bufs=1))
+        ring = ctx.enter_context(tc.tile_pool(name="ring", bufs=3))
+        psum = ctx.enter_context(tc.psum_pool(name="psum", bufs=8))
+
+        idx = lists.tile([P, S // 16], U16, name="idx")
+        idx2 = lists.tile([P, S2 // 16], U16, name="idx2")
+        p1 = lists.tile([P, NP // 16], U16, name="p1")
+        p2 = lists.tile([P, NP // 16], U16, name="p2")
+
+        def kept(shape, dtype, name, tag=None):
+            return keep.tile(shape, dtype, name=name, tag=tag or name, align_bytes=64)
+
+        ts = kept([P, T], U8, "ts")
+        vs_b = kept([P, S], U8, "vs_b")
+        w4s_raw = kept([P, 2, H], U8, "w4s_raw")
+        t2s = kept([P, T3], U8, "t2s")
+        nc.vector.memset(ts[:].bitcast(I32), 0)
+        nc.vector.memset(w4s_raw[:].rearrange("p a c -> p (a c)").bitcast(I32), 0)
+        nc.vector.memset(t2s[:].bitcast(I32), 0)
+        nc.vector.memset(vs_b[:].bitcast(I32), 0)
+
+        def load_words(src, columns, name, tag):
+            words = kept([P, columns], U32, name, tag)
+            nc.sync.dma_start(words[:].bitcast(I32), src.rearrange("p t i -> p (t i)").bitcast(I32))
+            return words
+
+        def load_w4(b):
+            raw = kept([P, 2, 2 * BANK], U8, f"w4_raw{b}")
+            nc.sync.dma_start(
+                raw[:].bitcast(I32),
+                w4_words[:, :, 2 * BANK * b : 2 * BANK * (b + 1)].rearrange("a p c -> p a c").bitcast(I32),
+            )
+            return raw
+
+        def load_w1(b):
+            raw = kept([P, PACK, BANK], F32, f"w1_raw{b}")
+            nc.sync.dma_start(raw[:], w1[:, BANK * b : BANK * (b + 1)].rearrange("(p j) c -> p j c", j=PACK))
+            return raw
+
+        def load_wish(b, t):
+            rows = kept([P, S], F32, f"h{b}{t}")
+            nc.sync.dma_start(rows[:], wish[BANK * b : BANK * (b + 1), :].rearrange("(p t) j -> p t j", t=PACK)[:, t, :])
+            return rows
+
+        def load_t2s(q):
+            nc.sync.dma_start(
+                t2s[32 * q + 8 : 32 * q + 16, :].bitcast(I32),
+                tab2_scales[:, 4 * q : 4 * q + 4, :].bitcast(I32),
+            )
+
+        nc.sync.dma_start(idx[:], offs)
+        nc.sync.dma_start(idx2[:], offs2)
+        nc.sync.dma_start(p1[:], pos1)
+        nc.sync.dma_start(p2[:], pos2)
+        gain_sb = kept([P, 2, PACK], F32, "gain_sb")
+        nc.sync.dma_start(gain_sb[:], gain.rearrange("(b p t) -> p b t", b=2, t=PACK))
+        w4_raw = [load_w4(0), load_w4(1)]
+        w1_raw = [load_w1(0)]
+        for q in range(QUADS):
+            nc.sync.dma_start(
+                ts[32 * q : 32 * q + 12, :].bitcast(I32),
+                tab_scales[:, 4 * q : 4 * q + 4, :].bitcast(I32),
+            )
+        tw = {0: load_words(tab_words[0], T, "tw0", "slot0")}
+        for q in range(QUADS):
+            nc.sync.dma_start(
+                w4s_raw[32 * q : 32 * q + 4, :, :].bitcast(I32),
+                w4_scales[:, 4 * q : 4 * q + 4, :].rearrange("a r c -> r a c").bitcast(I32),
+            )
+        tw[2] = load_words(tab_words[2], T, "tw2", "slot1")
+        load_t2s(0)
+        load_t2s(1)
+
+        vs = kept([P, S], U8, "vs")
+        v2s = kept([P, S2], U8, "v2s")
+        vw = [kept([P, S], U32, f"vw{a}") for a in range(3)]
+        nc.vector.tensor_copy(vs[:], ts[:].indirect(idx[:]))
+        for q in range(QUADS):
+            nc.sync.dma_start(vs_b[32 * q : 32 * q + 4, :].bitcast(I32), vs[32 * q + 4 : 32 * q + 8, :].bitcast(I32))
+        tw[1] = load_words(tab_words[1], T, "tw1", "slot2")
+        load_t2s(2)
+        load_t2s(3)
+        nc.vector.tensor_copy(vw[0][:], tw[0][:].indirect(idx[:]))
+        h = {}
+        h[0, 0] = load_wish(0, 0)
+
+        def deal_w4(b):
+            words = kept([P, 2, PACK, 2 * P], U8, f"w4_words{b}")
+            scales = kept([P, 2, PACK, P], U8, f"w4_scales{b}")
+            nc.vector.tensor_copy(
+                words[:].bitcast(U16),
+                w4_raw[b][:].bitcast(U16).rearrange("p a (q t) -> p a t q", t=PACK),
+            )
+            nc.vector.tensor_copy(
+                scales[:],
+                w4s_raw[:, :, BANK * b : BANK * (b + 1)].rearrange("p a (q t) -> p a t q", t=PACK),
+            )
+            return words, scales
+
+        def quantise_w1(b):
+            grouped = kept([P, PACK, P, PACK], BF16, f"w1_grouped{b}", "w1_grouped")
+            nc.scalar.activation(
+                out=grouped[:].rearrange("p t q j -> p q t j"),
+                in_=w1_raw[b][:].rearrange("p j (q t) -> p q t j", t=PACK),
+                func=ACT.Copy,
+            )
+            codes = kept([P, BANK], U32, f"w1_codes{b}")
+            scales = kept([P, BANK], U8, f"w1_scales{b}")
+            nc.vector.quantize_mx(
+                out=codes[:].bitcast(FP8X4), scales=scales[:], in_=grouped[:].rearrange("p t q j -> p (t q j)")
+            )
+            return codes, scales
+
+        w4 = [deal_w4(0)]
+        nc.vector.tensor_copy(vw[2][:], tw[2][:].indirect(idx[:]))
+        w1q = [quantise_w1(0)]
+        for half in range(2):
+            nc.vector.tensor_copy(
+                vw[1][:, BANK * half : BANK * (half + 1)], tw[1][:].indirect(idx[:, 32 * half : 32 * (half + 1)])
+            )
+        nc.vector.tensor_copy(v2s[:], t2s[:].indirect(idx2[:]))
+
+        h[0, 1] = load_wish(0, 1)
+        w1_raw.append(load_w1(1))
+        for t in range(2, PACK):
+            h[0, t] = load_wish(0, t)
+        for t in range(PACK - 1):
+            h[1, t] = load_wish(1, t)
+        t2w = [load_words(tab2_words[0], T3, "t2w0", "slot0")]
+        h[1, PACK - 1] = load_wish(1, PACK - 1)
+        t2w.append(load_words(tab2_words[1], T3, "t2w1", "slot1"))
+        festive_sb = kept([P, M_TILES], F32, "festive_sb")
+        favour_sb = kept([P, M_TILES], F32, "favour_sb")
+        with nc.allow_non_contiguous_dma(reason="one value a partition"):
+            nc.sync.dma_start(festive_sb[:], festive.rearrange("(m p) -> p m", p=P))
+            nc.sync.dma_start(favour_sb[:], favour.rearrange("(m p) -> p m", p=P))
+
+        starts = [sum(CHUNKS[:c]) for c in range(len(CHUNKS))]
+        def picked_tiles(c, b, tags):
+            return [kept([P, PACK, CHUNKS[c]], F32, f"picked_c{c}b{b}x{x}", tags[x]) for x in range(2)]
+
+        def pick(picked, c, b, t, x):
+            cols = slice(starts[c] // 16, (starts[c] + CHUNKS[c]) // 16)
+            nc.vector.tensor_copy(picked[x][:, t, :], h[b, t][:].indirect((p1, p2)[x][:, cols]))
+
+        def quantise_picked(picked, c, b, x):
+            n = CHUNKS[c]
+            grouped = ring.tile([P, n, PACK], BF16, name="x_grouped", align_bytes=64)
+            nc.scalar.activation(
+                out=grouped[:].rearrange("p (c i) t -> p c t i", i=PACK),
+                in_=picked[x][:].rearrange("p t (c i) -> p c t i", i=PACK),
+                func=(ACT.Copy, ACT.Abs)[x],
+            )
+            codes = kept([P, n], U32, f"x_codes{c}{b}{x}")
+            scales = kept([P, n], U8, f"x_scales{c}{b}{x}")
+            nc.vector.quantize_mx(
+                out=codes[:].bitcast(FP8X4), scales=scales[:], in_=grouped[:].rearrange("p n t -> p (n t)")
+            )
+            xq[c, b, x] = codes, scales
+
+        xq = {}
+        for b in range(2):
+            if b == 1:
+                w4.append(deal_w4(1))
+                w1q.append(quantise_w1(1))
+            banks = {}
+            for t in range(PACK):
+                for half in range(2):
+                    banks[t, half] = psum.tile([P, BANK], F32, name="bank")
+
+            def w4_pass(a, v_scales, t, half):
+                cols = slice(BANK * half, BANK * (half + 1))
+                nc.tensor.matmul_mx(
+                    out=banks[t, half][:],
+                    lhsT=w4[b][0][:, a, t, :].bitcast(FP4X4), lhsT_scale=w4[b][1][:, a, t, :],
+                    rhs=vw[a][:, cols].bitcast(FP8X4), rhs_scale=v_scales[:, cols],
+                    start=(a == 0), stop=(a == 1),
+                )
+
+            for t in range(PACK):
+                for half in range(2):
+                    w4_pass(0, vs, t, half)
+            for t in range(PACK):
+                rows = slice(P * t, P * (t + 1))
+                for half in range(2):
+                    cols = slice(BANK * half, BANK * (half + 1))
+                    nc.tensor.matmul_mx(
+                        out=banks[t, half][:],
+                        lhsT=w1q[b][0][:, rows].bitcast(FP8X4), lhsT_scale=w1q[b][1][:, rows],
+                        rhs=vw[2][:, cols].bitcast(FP8X4), rhs_scale=vs[8:P, cols],
+                        start=False, stop=False,
+                    )
+            picked = picked_tiles(0, b, (f"picked{b}0", f"picked{b}1"))
+            for t in range(PACK):
+                squashed = ring.tile([P, S], F32, name="squashed")
+                for half in range(2):
+                    cols = slice(BANK * half, BANK * (half + 1))
+                    w4_pass(1, vs_b, t, half)
+                    nc.scalar.activation(out=squashed[:, cols], in_=banks[t, half][:], func=ACT.Tanh)
+                nc.vector.scalar_tensor_tensor(
+                    out=h[b, t][:], in0=squashed[:], scalar=gain_sb[:, b, t : t + 1], in1=h[b, t][:],
+                    op0=ALU.mult, op1=ALU.add,
+                )
+                pick(picked, 0, b, t, 0)
+                pick(picked, 0, b, t, 1)
+            if b == 1:
+                v2w = [kept([P, S2], U32, f"v2w{a}") for a in range(2)]
+                for a in range(2):
+                    nc.vector.tensor_copy(v2w[a][:], t2w[a][:].indirect(idx2[:]))
+            for x in range(2):
+                quantise_picked(picked, 0, b, x)
+
+        out_view = out.rearrange("(m p) n -> p m n", p=P)
+
+        results = {}
+
+        def products(c, x):
+            n = CHUNKS[c]
+            per_bank = BANK // n
+            banks = [psum.tile([P, per_bank, n], F32, name="bank") for k in range(M_TILES // per_bank)]
+            for b in range(2):
+                for m in range(M_TILES):
+                    k, place = divmod(m, per_bank)
+                    cols = slice(P * m, P * (m + 1))
+                    nc.tensor.matmul_mx(
+                        out=banks[k][:, place, :],
+                        lhsT=v2w[b][:, cols].bitcast(FP8X4), lhsT_scale=v2s[8 + 4 * b : P, cols],
+                        rhs=xq[c, b, x][0][:].bitcast(FP8X4), rhs_scale=xq[c, b, x][1][:],
+                        start=(b == 0 and place == 0), stop=(b == 1 and place == per_bank - 1),
+                    )
+            return banks
+
+        def best_scores(c):
+            n = CHUNKS[c]
+            per_bank = BANK // n
+            e1, e2 = products(c, 0), products(c, 1)
+            results[c] = kept([P, M_TILES, n], F32, f"result{c}")
+            for k in range(len(e1)):
+                shifted = kept([P, per_bank, n], F32, f"shifted{c}{k}")
+                for place in range(per_bank):
+                    m = k * per_bank + place
+                    nc.scalar.activation(
+                        out=shifted[:, place, :], in_=e1[k][:, place, :], func=ACT.Identity,
+                        bias=festive_sb[:, m : m + 1],
+                    )
+                rows = slice(k * per_bank, (k + 1) * per_bank)
+                nc.vector.tensor_tensor(out=results[c][:, rows, :], in0=e2[k][:], in1=shifted[:], op=ALU.max)
+                weigh(c, rows)
+
+        def weigh(c, rows):
+            for m in range(rows.start, rows.stop):
+                if c == len(CHUNKS) - 1:
+                    nc.vector.tensor_scalar(
+                        out=results[c][:, m, :], in0=results[c][:, m, :], scalar1=favour_sb[:, m : m + 1],
+                        scalar2=None, op0=ALU.mult,
+                    )
+                else:
+                    nc.scalar.activation(
+                        out=results[c][:, m, :], in_=results[c][:, m, :], func=ACT.Copy, scale=favour_sb[:, m : m + 1]
+                    )
+            nc.sync.dma_start(out_view[:, rows, starts[c] : starts[c] + CHUNKS[c]], results[c][:, rows, :])
+
+        def pick_chunk(c, b, tags):
+            picked = picked_tiles(c, b, tags)
+            for x in range(2):
+                for t in range(PACK):
+                    pick(picked, c, b, t, x)
+                quantise_picked(picked, c, b, x)
+
+        pick_chunk(1, 0, ("slot1", "slot0"))
+        pick_chunk(1, 1, ("picked10", "picked11"))
+        best_scores(0)
+        best_scores(1)
+        pick_chunk(2, 0, ("shifted01", "shifted03"))
+        pick_chunk(2, 1, ("shifted10", "shifted11"))
+        best_scores(2)

@@ -1,6 +1,7 @@
 from contextlib import ExitStack
 
 import concourse.mybir as mybir
+from concourse.masks import make_identity
 
 F32 = mybir.dt.float32
 BF16 = mybir.dt.bfloat16
@@ -21,6 +22,8 @@ BANK = 512
 QUADS = 4
 M_TILES = S2 // P
 CHUNKS = (256, 128, 128)
+
+HOW = "VVVVVVVV"
 
 FLOPS = 2 * 1536 * H * S + 2 * 2 * H * S2 * NP
 
@@ -52,6 +55,11 @@ def tile_list_present_shortlist_scores_kernel(
         nc.vector.memset(w4s_raw[:].rearrange("p a c -> p (a c)").bitcast(I32), 0)
         nc.vector.memset(t2s[:].bitcast(I32), 0)
         nc.vector.memset(vs_b[:].bitcast(I32), 0)
+
+        toy_rows = kept([P, P], F32, "toy_rows")
+        identity = kept([P, P], F32, "identity")
+        nc.gpsimd.memset(toy_rows[:], 0.0)
+        make_identity(nc, identity[:])
 
         def load_words(src, columns, name, tag):
             words = kept([P, columns], U32, name, tag)
@@ -89,21 +97,25 @@ def tile_list_present_shortlist_scores_kernel(
         gain_sb = kept([P, 2, PACK], F32, "gain_sb")
         nc.sync.dma_start(gain_sb[:], gain.rearrange("(b p t) -> p b t", b=2, t=PACK))
         w4_raw = [load_w4(0), load_w4(1)]
-        w1_raw = [load_w1(0)]
+        tw = {0: load_words(tab_words[0], T, "tw0", "slot0")}
         for q in range(QUADS):
             nc.sync.dma_start(
                 ts[32 * q : 32 * q + 12, :].bitcast(I32),
                 tab_scales[:, 4 * q : 4 * q + 4, :].bitcast(I32),
             )
-        tw = {0: load_words(tab_words[0], T, "tw0", "slot0")}
+        tw[2] = load_words(tab_words[2], T, "tw2", "slot1")
         for q in range(QUADS):
             nc.sync.dma_start(
                 w4s_raw[32 * q : 32 * q + 4, :, :].bitcast(I32),
                 w4_scales[:, 4 * q : 4 * q + 4, :].rearrange("a r c -> r a c").bitcast(I32),
             )
-        tw[2] = load_words(tab_words[2], T, "tw2", "slot1")
-        load_t2s(0)
-        load_t2s(1)
+        w1_raw = [load_w1(0)]
+        nc.sync.dma_start(toy_rows[0:M_TILES, :], festive.rearrange("(m p) -> m p", p=P))
+        nc.sync.dma_start(toy_rows[M_TILES : 2 * M_TILES, :], favour.rearrange("(m p) -> m p", p=P))
+        turned = psum.tile([P, P], F32, name="bank")
+        nc.tensor.transpose(turned[:], toy_rows[:], identity[:])
+        toy_columns = kept([P, 2, M_TILES], F32, "toy_columns")
+        nc.scalar.copy(toy_columns[:].rearrange("p v m -> p (v m)"), turned[:, 0 : 2 * M_TILES])
 
         vs = kept([P, S], U8, "vs")
         v2s = kept([P, S2], U8, "v2s")
@@ -112,11 +124,8 @@ def tile_list_present_shortlist_scores_kernel(
         for q in range(QUADS):
             nc.sync.dma_start(vs_b[32 * q : 32 * q + 4, :].bitcast(I32), vs[32 * q + 4 : 32 * q + 8, :].bitcast(I32))
         tw[1] = load_words(tab_words[1], T, "tw1", "slot2")
-        load_t2s(2)
-        load_t2s(3)
         nc.vector.tensor_copy(vw[0][:], tw[0][:].indirect(idx[:]))
         h = {}
-        h[0, 0] = load_wish(0, 0)
 
         def deal_w4(b):
             words = kept([P, 2, PACK, 2 * P], U8, f"w4_words{b}")
@@ -152,45 +161,45 @@ def tile_list_present_shortlist_scores_kernel(
             nc.vector.tensor_copy(
                 vw[1][:, BANK * half : BANK * (half + 1)], tw[1][:].indirect(idx[:, 32 * half : 32 * (half + 1)])
             )
-        nc.vector.tensor_copy(v2s[:], t2s[:].indirect(idx2[:]))
-
+        t2w = {}
+        h[0, 0] = load_wish(0, 0)
+        for q in range(QUADS):
+            load_t2s(q)
         h[0, 1] = load_wish(0, 1)
         w1_raw.append(load_w1(1))
-        for t in range(2, PACK):
-            h[0, t] = load_wish(0, t)
-        for t in range(PACK - 1):
-            h[1, t] = load_wish(1, t)
-        t2w = [load_words(tab2_words[0], T3, "t2w0", "slot0")]
-        h[1, PACK - 1] = load_wish(1, PACK - 1)
-        t2w.append(load_words(tab2_words[1], T3, "t2w1", "slot1"))
-        festive_sb = kept([P, M_TILES], F32, "festive_sb")
-        favour_sb = kept([P, M_TILES], F32, "favour_sb")
-        with nc.allow_non_contiguous_dma(reason="one value a partition"):
-            nc.sync.dma_start(festive_sb[:], festive.rearrange("(m p) -> p m", p=P))
-            nc.sync.dma_start(favour_sb[:], favour.rearrange("(m p) -> p m", p=P))
+        h[0, 2] = load_wish(0, 2)
+        h[0, 3] = load_wish(0, 3)
+        h[1, 0] = load_wish(1, 0)
+        t2w[0] = load_words(tab2_words[0], T3, "t2w0", "slot0")
+        h[1, 1] = load_wish(1, 1)
+        h[1, 2] = load_wish(1, 2)
+        h[1, 3] = load_wish(1, 3)
+        t2w[1] = load_words(tab2_words[1], T3, "t2w1", "slot1")
+        nc.vector.tensor_copy(v2s[:], t2s[:].indirect(idx2[:]))
+
 
         starts = [sum(CHUNKS[:c]) for c in range(len(CHUNKS))]
-        def picked_tiles(c, b, tags):
-            return [kept([P, PACK, CHUNKS[c]], F32, f"picked_c{c}b{b}x{x}", tags[x]) for x in range(2)]
+        def picked_tiles(name, n, tags):
+            return [kept([P, PACK, n], F32, f"picked_{name}x{x}", tags[x]) for x in range(2)]
 
-        def pick(picked, c, b, t, x):
-            cols = slice(starts[c] // 16, (starts[c] + CHUNKS[c]) // 16)
+        def pick(picked, start, b, t, x):
+            cols = slice(start // 16, (start + picked[x].shape[2]) // 16)
             nc.vector.tensor_copy(picked[x][:, t, :], h[b, t][:].indirect((p1, p2)[x][:, cols]))
 
-        def quantise_picked(picked, c, b, x):
-            n = CHUNKS[c]
-            grouped = ring.tile([P, n, PACK], BF16, name="x_grouped", align_bytes=64)
+        def quantise_picked(picked, name, x):
+            n = picked[x].shape[2]
+            grouped = ring.tile([P, n, PACK], BF16, name="x_grouped", align_bytes=64, bufs=2)
             nc.scalar.activation(
                 out=grouped[:].rearrange("p (c i) t -> p c t i", i=PACK),
                 in_=picked[x][:].rearrange("p t (c i) -> p c t i", i=PACK),
                 func=(ACT.Copy, ACT.Abs)[x],
             )
-            codes = kept([P, n], U32, f"x_codes{c}{b}{x}")
-            scales = kept([P, n], U8, f"x_scales{c}{b}{x}")
+            codes = kept([P, n], U32, f"x_codes{name}{x}")
+            scales = kept([P, n], U8, f"x_scales{name}{x}")
             nc.vector.quantize_mx(
                 out=codes[:].bitcast(FP8X4), scales=scales[:], in_=grouped[:].rearrange("p n t -> p (n t)")
             )
-            xq[c, b, x] = codes, scales
+            return codes, scales
 
         xq = {}
         for b in range(2):
@@ -202,39 +211,46 @@ def tile_list_present_shortlist_scores_kernel(
                 for half in range(2):
                     banks[t, half] = psum.tile([P, BANK], F32, name="bank")
 
-            def w4_pass(a, v_scales, t, half):
+            def stage_one_pass(a, t, half, start, stop):
                 cols = slice(BANK * half, BANK * (half + 1))
+                if a < 2:
+                    weights, weight_scales = w4[b][0][:, a, t, :].bitcast(FP4X4), w4[b][1][:, a, t, :]
+                else:
+                    rows = slice(P * t, P * (t + 1))
+                    weights, weight_scales = w1q[b][0][:, rows].bitcast(FP8X4), w1q[b][1][:, rows]
                 nc.tensor.matmul_mx(
-                    out=banks[t, half][:],
-                    lhsT=w4[b][0][:, a, t, :].bitcast(FP4X4), lhsT_scale=w4[b][1][:, a, t, :],
-                    rhs=vw[a][:, cols].bitcast(FP8X4), rhs_scale=v_scales[:, cols],
-                    start=(a == 0), stop=(a == 1),
+                    out=banks[t, half][:], lhsT=weights, lhsT_scale=weight_scales,
+                    rhs=vw[a][:, cols].bitcast(FP8X4), rhs_scale=(vs[:, cols], vs_b[:, cols], vs[8:P, cols])[a],
+                    start=start, stop=stop,
                 )
 
-            for t in range(PACK):
-                for half in range(2):
-                    w4_pass(0, vs, t, half)
-            for t in range(PACK):
-                rows = slice(P * t, P * (t + 1))
-                for half in range(2):
-                    cols = slice(BANK * half, BANK * (half + 1))
-                    nc.tensor.matmul_mx(
-                        out=banks[t, half][:],
-                        lhsT=w1q[b][0][:, rows].bitcast(FP8X4), lhsT_scale=w1q[b][1][:, rows],
-                        rhs=vw[2][:, cols].bitcast(FP8X4), rhs_scale=vs[8:P, cols],
-                        start=False, stop=False,
-                    )
-            picked = picked_tiles(0, b, (f"picked{b}0", f"picked{b}1"))
+            first, second, final = ((0, 2, 1), (0, 1, 2))[b]
+            for a in (first, second):
+                for t in range(PACK):
+                    for half in range(2):
+                        stage_one_pass(a, t, half, a == first, False)
+            picked = picked_tiles(f"b{b}", (NP, CHUNKS[0])[b], (("slot2", "picked01"), ("picked10", "picked11"))[b])
             for t in range(PACK):
                 squashed = ring.tile([P, S], F32, name="squashed")
                 for half in range(2):
                     cols = slice(BANK * half, BANK * (half + 1))
-                    w4_pass(1, vs_b, t, half)
+                    stage_one_pass(final, t, half, False, True)
                     nc.scalar.activation(out=squashed[:, cols], in_=banks[t, half][:], func=ACT.Tanh)
-                nc.vector.scalar_tensor_tensor(
-                    out=h[b, t][:], in0=squashed[:], scalar=gain_sb[:, b, t : t + 1], in1=h[b, t][:],
-                    op0=ALU.mult, op1=ALU.add,
-                )
+                how = HOW[PACK * b + t]
+                if how == "V":
+                    nc.vector.scalar_tensor_tensor(
+                        out=h[b, t][:], in0=squashed[:], scalar=gain_sb[:, b, t : t + 1], in1=h[b, t][:],
+                        op0=ALU.mult, op1=ALU.add,
+                    )
+                else:
+                    if how == "S":
+                        nc.scalar.activation(out=squashed[:], in_=squashed[:], func=ACT.Copy, scale=gain_sb[:, b, t : t + 1])
+                    else:
+                        nc.gpsimd.tensor_scalar(
+                            out=squashed[:], in0=squashed[:], scalar1=gain_sb[:, b, t : t + 1], scalar2=0.0,
+                            op0=ALU.mult, op1=ALU.add,
+                        )
+                    nc.gpsimd.tensor_tensor(out=h[b, t][:], in0=squashed[:], in1=h[b, t][:], op=ALU.add)
                 pick(picked, 0, b, t, 0)
                 pick(picked, 0, b, t, 1)
             if b == 1:
@@ -242,7 +258,12 @@ def tile_list_present_shortlist_scores_kernel(
                 for a in range(2):
                     nc.vector.tensor_copy(v2w[a][:], t2w[a][:].indirect(idx2[:]))
             for x in range(2):
-                quantise_picked(picked, 0, b, x)
+                codes, scales = quantise_picked(picked, f"b{b}", x)
+                if b == 0:
+                    for c, n in enumerate(CHUNKS):
+                        xq[c, 0, x] = codes[:, starts[c] : starts[c] + n], scales[:, starts[c] : starts[c] + n]
+                else:
+                    xq[0, 1, x] = codes[:], scales[:]
 
         out_view = out.rearrange("(m p) n -> p m n", p=P)
 
@@ -259,7 +280,7 @@ def tile_list_present_shortlist_scores_kernel(
                     nc.tensor.matmul_mx(
                         out=banks[k][:, place, :],
                         lhsT=v2w[b][:, cols].bitcast(FP8X4), lhsT_scale=v2s[8 + 4 * b : P, cols],
-                        rhs=xq[c, b, x][0][:].bitcast(FP8X4), rhs_scale=xq[c, b, x][1][:],
+                        rhs=xq[c, b, x][0].bitcast(FP8X4), rhs_scale=xq[c, b, x][1],
                         start=(b == 0 and place == 0), stop=(b == 1 and place == per_bank - 1),
                     )
             return banks
@@ -275,7 +296,7 @@ def tile_list_present_shortlist_scores_kernel(
                     m = k * per_bank + place
                     nc.scalar.activation(
                         out=shifted[:, place, :], in_=e1[k][:, place, :], func=ACT.Identity,
-                        bias=festive_sb[:, m : m + 1],
+                        bias=toy_columns[:, 0, m : m + 1],
                     )
                 rows = slice(k * per_bank, (k + 1) * per_bank)
                 nc.vector.tensor_tensor(out=results[c][:, rows, :], in0=e2[k][:], in1=shifted[:], op=ALU.max)
@@ -283,28 +304,32 @@ def tile_list_present_shortlist_scores_kernel(
 
         def weigh(c, rows):
             for m in range(rows.start, rows.stop):
-                if c == len(CHUNKS) - 1:
+                if c == len(CHUNKS) - 1 and rows.start == 0:
+                    nc.scalar.activation(
+                        out=results[c][:, m, :], in_=results[c][:, m, :], func=ACT.Copy, scale=toy_columns[:, 1, m : m + 1]
+                    )
+                elif c == len(CHUNKS) - 1:
                     nc.vector.tensor_scalar(
-                        out=results[c][:, m, :], in0=results[c][:, m, :], scalar1=favour_sb[:, m : m + 1],
+                        out=results[c][:, m, :], in0=results[c][:, m, :], scalar1=toy_columns[:, 1, m : m + 1],
                         scalar2=None, op0=ALU.mult,
                     )
                 else:
-                    nc.scalar.activation(
-                        out=results[c][:, m, :], in_=results[c][:, m, :], func=ACT.Copy, scale=favour_sb[:, m : m + 1]
+                    nc.gpsimd.tensor_scalar(
+                        out=results[c][:, m, :], in0=results[c][:, m, :], scalar1=toy_columns[:, 1, m : m + 1],
+                        scalar2=0.0, op0=ALU.mult, op1=ALU.add,
                     )
             nc.sync.dma_start(out_view[:, rows, starts[c] : starts[c] + CHUNKS[c]], results[c][:, rows, :])
 
-        def pick_chunk(c, b, tags):
-            picked = picked_tiles(c, b, tags)
+        def pick_chunk(c, tags):
+            picked = picked_tiles(f"c{c}", CHUNKS[c], tags)
             for x in range(2):
                 for t in range(PACK):
-                    pick(picked, c, b, t, x)
-                quantise_picked(picked, c, b, x)
+                    pick(picked, starts[c], 1, t, x)
+                codes, scales = quantise_picked(picked, f"c{c}", x)
+                xq[c, 1, x] = codes[:], scales[:]
 
-        pick_chunk(1, 0, ("slot1", "slot0"))
-        pick_chunk(1, 1, ("picked10", "picked11"))
+        pick_chunk(1, ("slot1","picked10"))
         best_scores(0)
         best_scores(1)
-        pick_chunk(2, 0, ("shifted01", "shifted03"))
-        pick_chunk(2, 1, ("shifted10", "shifted11"))
+        pick_chunk(2, ("shifted01","shifted03"))
         best_scores(2)

@@ -23,7 +23,7 @@ QUADS = 4
 M_TILES = S2 // P
 CHUNKS = (256, 128, 128)
 
-HOW = "VVVVVVVV"
+HOW = "VVSSSSSS"
 
 FLOPS = 2 * 1536 * H * S + 2 * 2 * H * S2 * NP
 
@@ -165,13 +165,13 @@ def tile_list_present_shortlist_scores_kernel(
         h[0, 0] = load_wish(0, 0)
         for q in range(QUADS):
             load_t2s(q)
-        h[0, 1] = load_wish(0, 1)
         w1_raw.append(load_w1(1))
+        h[0, 1] = load_wish(0, 1)
         h[0, 2] = load_wish(0, 2)
         h[0, 3] = load_wish(0, 3)
         h[1, 0] = load_wish(1, 0)
-        t2w[0] = load_words(tab2_words[0], T3, "t2w0", "slot0")
         h[1, 1] = load_wish(1, 1)
+        t2w[0] = load_words(tab2_words[0], T3, "t2w0", "slot0")
         h[1, 2] = load_wish(1, 2)
         h[1, 3] = load_wish(1, 3)
         t2w[1] = load_words(tab2_words[1], T3, "t2w1", "slot1")
@@ -202,10 +202,10 @@ def tile_list_present_shortlist_scores_kernel(
             return codes, scales
 
         xq = {}
+        w4.append(deal_w4(1))
+        w1q.append(quantise_w1(1))
+        picked_by_half = {}
         for b in range(2):
-            if b == 1:
-                w4.append(deal_w4(1))
-                w1q.append(quantise_w1(1))
             banks = {}
             for t in range(PACK):
                 for half in range(2):
@@ -231,7 +231,7 @@ def tile_list_present_shortlist_scores_kernel(
                         stage_one_pass(a, t, half, a == first, False)
             picked = picked_tiles(f"b{b}", (NP, CHUNKS[0])[b], (("slot2", "picked01"), ("picked10", "picked11"))[b])
             for t in range(PACK):
-                squashed = ring.tile([P, S], F32, name="squashed")
+                squashed = ring.tile([P, S], F32, name="squashed", bufs=3)
                 for half in range(2):
                     cols = slice(BANK * half, BANK * (half + 1))
                     stage_one_pass(final, t, half, False, True)
@@ -253,18 +253,20 @@ def tile_list_present_shortlist_scores_kernel(
                     nc.gpsimd.tensor_tensor(out=h[b, t][:], in0=squashed[:], in1=h[b, t][:], op=ALU.add)
                 pick(picked, 0, b, t, 0)
                 pick(picked, 0, b, t, 1)
+                picked_by_half[b] = picked
+                if b == 1 and t == 3:
+                    for x in range(2):
+                        codes, scales = quantise_picked(picked_by_half[0], "b0", x)
+                        for c, n in enumerate(CHUNKS):
+                            xq[c, 0, x] = codes[:, starts[c] : starts[c] + n], scales[:, starts[c] : starts[c] + n]
             if b == 1:
                 v2w = [kept([P, S2], U32, f"v2w{a}") for a in range(2)]
                 for a in range(2):
                     nc.vector.tensor_copy(v2w[a][:], t2w[a][:].indirect(idx2[:]))
-            for x in range(2):
-                codes, scales = quantise_picked(picked, f"b{b}", x)
-                if b == 0:
-                    for c, n in enumerate(CHUNKS):
-                        xq[c, 0, x] = codes[:, starts[c] : starts[c] + n], scales[:, starts[c] : starts[c] + n]
-                else:
-                    xq[0, 1, x] = codes[:], scales[:]
 
+        for x in range(2):
+            codes, scales = quantise_picked(picked_by_half[1], "b1", x)
+            xq[0, 1, x] = codes[:], scales[:]
         out_view = out.rearrange("(m p) n -> p m n", p=P)
 
         results = {}

@@ -48,13 +48,15 @@ def tile_list_present_shortlist_scores_kernel(
             return keep.tile(shape, dtype, name=name, tag=tag or name, align_bytes=64)
 
         ts = kept([P, T], U8, "ts")
-        vs_b = kept([P, S], U8, "vs_b")
+        planes = kept([P, 3, S], U8, "planes")
+        planes2 = kept([P, 2, S2], U8, "planes2")
         w4s_raw = kept([P, 2, H], U8, "w4s_raw")
         t2s = kept([P, T3], U8, "t2s")
         nc.vector.memset(ts[:].bitcast(I32), 0)
-        nc.vector.memset(w4s_raw[:].rearrange("p a c -> p (a c)").bitcast(I32), 0)
         nc.vector.memset(t2s[:].bitcast(I32), 0)
-        nc.vector.memset(vs_b[:].bitcast(I32), 0)
+        nc.vector.memset(w4s_raw[:].rearrange("p a c -> p (a c)").bitcast(I32), 0)
+        nc.vector.memset(planes[:].rearrange("p a s -> p (a s)").bitcast(I32), 0)
+        nc.vector.memset(planes2[:].rearrange("p a s -> p (a s)").bitcast(I32), 0)
 
         toy_rows = kept([P, P], F32, "toy_rows")
         identity = kept([P, P], F32, "identity")
@@ -84,12 +86,6 @@ def tile_list_present_shortlist_scores_kernel(
             nc.sync.dma_start(rows[:], wish[BANK * b : BANK * (b + 1), :].rearrange("(p t) j -> p t j", t=PACK)[:, t, :])
             return rows
 
-        def load_t2s(q):
-            nc.sync.dma_start(
-                t2s[32 * q + 8 : 32 * q + 16, :].bitcast(I32),
-                tab2_scales[:, 4 * q : 4 * q + 4, :].bitcast(I32),
-            )
-
         nc.sync.dma_start(idx[:], offs)
         nc.sync.dma_start(idx2[:], offs2)
         nc.sync.dma_start(p1[:], pos1)
@@ -97,19 +93,16 @@ def tile_list_present_shortlist_scores_kernel(
         gain_sb = kept([P, 2, PACK], F32, "gain_sb")
         nc.sync.dma_start(gain_sb[:], gain.rearrange("(b p t) -> p b t", b=2, t=PACK))
         w4_raw = [load_w4(0), load_w4(1)]
+        w1_raw = [load_w1(0)]
+        nc.sync.dma_start(ts[0:96:2, :].bitcast(I32), tab_scales.rearrange("a q t -> q a t").bitcast(I32))
+        nc.sync.dma_start(t2s[0:P:4, :].bitcast(I32), tab2_scales.rearrange("a q t -> q a t").bitcast(I32))
         tw = {0: load_words(tab_words[0], T, "tw0", "slot0")}
-        for q in range(QUADS):
-            nc.sync.dma_start(
-                ts[32 * q : 32 * q + 12, :].bitcast(I32),
-                tab_scales[:, 4 * q : 4 * q + 4, :].bitcast(I32),
-            )
-        tw[2] = load_words(tab_words[2], T, "tw2", "slot1")
         for q in range(QUADS):
             nc.sync.dma_start(
                 w4s_raw[32 * q : 32 * q + 4, :, :].bitcast(I32),
                 w4_scales[:, 4 * q : 4 * q + 4, :].rearrange("a r c -> r a c").bitcast(I32),
             )
-        w1_raw = [load_w1(0)]
+        tw[2] = load_words(tab_words[2], T, "tw2", "slot1")
         nc.sync.dma_start(toy_rows[0:M_TILES, :], festive.rearrange("(m p) -> m p", p=P))
         nc.sync.dma_start(toy_rows[M_TILES : 2 * M_TILES, :], favour.rearrange("(m p) -> m p", p=P))
         turned = psum.tile([P, P], F32, name="bank")
@@ -121,8 +114,9 @@ def tile_list_present_shortlist_scores_kernel(
         v2s = kept([P, S2], U8, "v2s")
         vw = [kept([P, S], U32, f"vw{a}") for a in range(3)]
         nc.vector.tensor_copy(vs[:], ts[:].indirect(idx[:]))
+        nc.vector.tensor_copy(v2s[:], t2s[:].indirect(idx2[:]))
         for q in range(QUADS):
-            nc.sync.dma_start(vs_b[32 * q : 32 * q + 4, :].bitcast(I32), vs[32 * q + 4 : 32 * q + 8, :].bitcast(I32))
+            nc.sync.dma_start(planes[32 * q : 32 * q + 4, :, :].bitcast(I32), vs[24 * q : 24 * q + 24 : 2, :].bitcast(I32))
         tw[1] = load_words(tab_words[1], T, "tw1", "slot2")
         nc.vector.tensor_copy(vw[0][:], tw[0][:].indirect(idx[:]))
         h = {}
@@ -163,24 +157,23 @@ def tile_list_present_shortlist_scores_kernel(
             )
         t2w = {}
         h[0, 0] = load_wish(0, 0)
-        for q in range(QUADS):
-            load_t2s(q)
         w1_raw.append(load_w1(1))
         h[0, 1] = load_wish(0, 1)
         h[0, 2] = load_wish(0, 2)
         h[0, 3] = load_wish(0, 3)
+        t2w[0] = load_words(tab2_words[0], T3, "t2w0", "slot0")
         h[1, 0] = load_wish(1, 0)
         h[1, 1] = load_wish(1, 1)
-        t2w[0] = load_words(tab2_words[0], T3, "t2w0", "slot0")
+        for q in range(QUADS):
+            nc.sync.dma_start(planes2[32 * q : 32 * q + 4, :, :].bitcast(I32), v2s[32 * q : 32 * q + 32 : 4, :].bitcast(I32))
         h[1, 2] = load_wish(1, 2)
         h[1, 3] = load_wish(1, 3)
         t2w[1] = load_words(tab2_words[1], T3, "t2w1", "slot1")
-        nc.vector.tensor_copy(v2s[:], t2s[:].indirect(idx2[:]))
 
 
         starts = [sum(CHUNKS[:c]) for c in range(len(CHUNKS))]
         def picked_tiles(name, n, tags):
-            return [kept([P, PACK, n], F32, f"picked_{name}x{x}", tags[x]) for x in range(2)]
+            return [kept([P, PACK, n], (BF16, F32)[x], f"picked_{name}x{x}", tags[x]) for x in range(2)]
 
         def pick(picked, start, b, t, x):
             cols = slice(start // 16, (start + picked[x].shape[2]) // 16)
@@ -189,11 +182,12 @@ def tile_list_present_shortlist_scores_kernel(
         def quantise_picked(picked, name, x):
             n = picked[x].shape[2]
             grouped = ring.tile([P, n, PACK], BF16, name="x_grouped", align_bytes=64, bufs=2)
-            nc.scalar.activation(
-                out=grouped[:].rearrange("p (c i) t -> p c t i", i=PACK),
-                in_=picked[x][:].rearrange("p t (c i) -> p c t i", i=PACK),
-                func=(ACT.Copy, ACT.Abs)[x],
-            )
+            regrouped = grouped[:].rearrange("p (c i) t -> p c t i", i=PACK)
+            source = picked[x][:].rearrange("p t (c i) -> p c t i", i=PACK)
+            if x == 0:
+                nc.scalar.copy(regrouped, source)
+            else:
+                nc.scalar.activation(out=regrouped, in_=source, func=ACT.Abs)
             codes = kept([P, n], U32, f"x_codes{name}{x}")
             scales = kept([P, n], U8, f"x_scales{name}{x}")
             nc.vector.quantize_mx(
@@ -220,7 +214,7 @@ def tile_list_present_shortlist_scores_kernel(
                     weights, weight_scales = w1q[b][0][:, rows].bitcast(FP8X4), w1q[b][1][:, rows]
                 nc.tensor.matmul_mx(
                     out=banks[t, half][:], lhsT=weights, lhsT_scale=weight_scales,
-                    rhs=vw[a][:, cols].bitcast(FP8X4), rhs_scale=(vs[:, cols], vs_b[:, cols], vs[8:P, cols])[a],
+                    rhs=vw[a][:, cols].bitcast(FP8X4), rhs_scale=planes[:, a, cols],
                     start=start, stop=stop,
                 )
 
@@ -238,10 +232,11 @@ def tile_list_present_shortlist_scores_kernel(
                     nc.scalar.activation(out=squashed[:, cols], in_=banks[t, half][:], func=ACT.Tanh)
                 how = HOW[PACK * b + t]
                 if how == "V":
-                    nc.vector.scalar_tensor_tensor(
-                        out=h[b, t][:], in0=squashed[:], scalar=gain_sb[:, b, t : t + 1], in1=h[b, t][:],
-                        op0=ALU.mult, op1=ALU.add,
-                    )
+                    for cols in (slice(0, BANK), slice(BANK, S)):
+                        nc.vector.scalar_tensor_tensor(
+                            out=h[b, t][:, cols], in0=squashed[:, cols], scalar=gain_sb[:, b, t : t + 1],
+                            in1=h[b, t][:, cols], op0=ALU.mult, op1=ALU.add,
+                        )
                 else:
                     if how == "S":
                         nc.scalar.activation(out=squashed[:], in_=squashed[:], func=ACT.Copy, scale=gain_sb[:, b, t : t + 1])
@@ -281,7 +276,7 @@ def tile_list_present_shortlist_scores_kernel(
                     cols = slice(P * m, P * (m + 1))
                     nc.tensor.matmul_mx(
                         out=banks[k][:, place, :],
-                        lhsT=v2w[b][:, cols].bitcast(FP8X4), lhsT_scale=v2s[8 + 4 * b : P, cols],
+                        lhsT=v2w[b][:, cols].bitcast(FP8X4), lhsT_scale=planes2[:, b, cols],
                         rhs=xq[c, b, x][0].bitcast(FP8X4), rhs_scale=xq[c, b, x][1],
                         start=(b == 0 and place == 0), stop=(b == 1 and place == per_bank - 1),
                     )

from contextlib import ExitStack

import concourse.mybir as mybir
from concourse.masks import make_identity

F32 = mybir.dt.float32
BF16 = mybir.dt.bfloat16
I32 = mybir.dt.int32
U32 = mybir.dt.uint32
U16 = mybir.dt.uint16
U8 = mybir.dt.uint8
FP8X4 = mybir.dt.float8_e4m3fn_x4
FP4X4 = mybir.dt.float4_e2m1fn_x4
ACT = mybir.ActivationFunctionType
ALU = mybir.AluOpType

P = 128
PACK = 4
T, T3 = 4096, 2048
H, S, S2, NP = 1024, 1024, 1024, 512
BANK = 512
QUADS = 4
M_TILES = S2 // P
CHUNKS = (256, 128, 128)

HOW = "VVSSSSSS"

FLOPS = 2 * 1536 * H * S + 2 * 2 * H * S2 * NP


def tile_list_present_shortlist_scores_kernel(
    tc, tab_words, tab_scales, offs, w4_words, w4_scales, w1, gain, wish,
    tab2_words, tab2_scales, offs2, pos1, pos2, festive, favour, out,
):
    nc = tc.nc
    with ExitStack() as ctx:
        lists = ctx.enter_context(tc.tile_pool(name="lists", bufs=1))
        keep = ctx.enter_context(tc.tile_pool(name="keep", bufs=1))
        ring = ctx.enter_context(tc.tile_pool(name="ring", bufs=3))
        psum = ctx.enter_context(tc.psum_pool(name="psum", bufs=8))

        idx = lists.tile([P, S // 16], U16, name="idx")
        idx2 = lists.tile([P, S2 // 16], U16, name="idx2")
        p1 = lists.tile([P, NP // 16], U16, name="p1")
        p2 = lists.tile([P, NP // 16], U16, name="p2")

        def kept(shape, dtype, name, tag=None):
            return keep.tile(shape, dtype, name=name, tag=tag or name, align_bytes=64)

        ts = kept([P, T], U8, "ts")
        planes = kept([P, 3, S], U8, "planes")
        planes2 = kept([P, 2, S2], U8, "planes2")
        w4s_raw = kept([P, 2, H], U8, "w4s_raw")
        t2s = kept([P, T3], U8, "t2s")
        nc.vector.memset(ts[:].bitcast(I32), 0)
        nc.vector.memset(t2s[:].bitcast(I32), 0)
        nc.vector.memset(w4s_raw[:].rearrange("p a c -> p (a c)").bitcast(I32), 0)
        nc.vector.memset(planes[:].rearrange("p a s -> p (a s)").bitcast(I32), 0)
        nc.vector.memset(planes2[:].rearrange("p a s -> p (a s)").bitcast(I32), 0)

        toy_rows = kept([P, P], F32, "toy_rows")
        identity = kept([P, P], F32, "identity")
        nc.gpsimd.memset(toy_rows[:], 0.0)
        make_identity(nc, identity[:])

        def load_words(src, columns, name, tag):
            words = kept([P, columns], U32, name, tag)
            nc.sync.dma_start(words[:].bitcast(I32), src.rearrange("p t i -> p (t i)").bitcast(I32))
            return words

        def load_w4(b):
            raw = kept([P, 2, 2 * BANK], U8, f"w4_raw{b}")
            nc.sync.dma_start(
                raw[:].bitcast(I32),
                w4_words[:, :, 2 * BANK * b : 2 * BANK * (b + 1)].rearrange("a p c -> p a c").bitcast(I32),
            )
            return raw

        def load_w1(b):
            raw = kept([P, PACK, BANK], F32, f"w1_raw{b}")
            nc.sync.dma_start(raw[:], w1[:, BANK * b : BANK * (b + 1)].rearrange("(p j) c -> p j c", j=PACK))
            return raw

        def load_wish(b, t):
            rows = kept([P, S], F32, f"h{b}{t}")
            nc.sync.dma_start(rows[:], wish[BANK * b : BANK * (b + 1), :].rearrange("(p t) j -> p t j", t=PACK)[:, t, :])
            return rows

        nc.sync.dma_start(idx[:], offs)
        nc.sync.dma_start(idx2[:], offs2)
        nc.sync.dma_start(p1[:], pos1)
        nc.sync.dma_start(p2[:], pos2)
        gain_sb = kept([P, 2, PACK], F32, "gain_sb")
        nc.sync.dma_start(gain_sb[:], gain.rearrange("(b p t) -> p b t", b=2, t=PACK))
        w4_raw = [load_w4(0), load_w4(1)]
        w1_raw = [load_w1(0)]
        nc.sync.dma_start(ts[0:96:2, :].bitcast(I32), tab_scales.rearrange("a q t -> q a t").bitcast(I32))
        nc.sync.dma_start(t2s[0:P:4, :].bitcast(I32), tab2_scales.rearrange("a q t -> q a t").bitcast(I32))
        tw = {0: load_words(tab_words[0], T, "tw0", "slot0")}
        for q in range(QUADS):
            nc.sync.dma_start(
                w4s_raw[32 * q : 32 * q + 4, :, :].bitcast(I32),
                w4_scales[:, 4 * q : 4 * q + 4, :].rearrange("a r c -> r a c").bitcast(I32),
            )
        tw[2] = load_words(tab_words[2], T, "tw2", "slot1")
        nc.sync.dma_start(toy_rows[0:M_TILES, :], festive.rearrange("(m p) -> m p", p=P))
        nc.sync.dma_start(toy_rows[M_TILES : 2 * M_TILES, :], favour.rearrange("(m p) -> m p", p=P))
        turned = psum.tile([P, P], F32, name="bank")
        nc.tensor.transpose(turned[:], toy_rows[:], identity[:])
        toy_columns = kept([P, 2, M_TILES], F32, "toy_columns")
        nc.scalar.copy(toy_columns[:].rearrange("p v m -> p (v m)"), turned[:, 0 : 2 * M_TILES])

        vs = kept([P, S], U8, "vs")
        v2s = kept([P, S2], U8, "v2s")
        vw = [kept([P, S], U32, f"vw{a}") for a in range(3)]
        nc.vector.tensor_copy(vs[:], ts[:].indirect(idx[:]))
        nc.vector.tensor_copy(v2s[:], t2s[:].indirect(idx2[:]))
        for q in range(QUADS):
            nc.sync.dma_start(planes[32 * q : 32 * q + 4, :, :].bitcast(I32), vs[24 * q : 24 * q + 24 : 2, :].bitcast(I32))
        tw[1] = load_words(tab_words[1], T, "tw1", "slot2")
        nc.vector.tensor_copy(vw[0][:], tw[0][:].indirect(idx[:]))
        h = {}

        def deal_w4(b):
            words = kept([P, 2, PACK, 2 * P], U8, f"w4_words{b}")
            scales = kept([P, 2, PACK, P], U8, f"w4_scales{b}")
            nc.vector.tensor_copy(
                words[:].bitcast(U16),
                w4_raw[b][:].bitcast(U16).rearrange("p a (q t) -> p a t q", t=PACK),
            )
            nc.vector.tensor_copy(
                scales[:],
                w4s_raw[:, :, BANK * b : BANK * (b + 1)].rearrange("p a (q t) -> p a t q", t=PACK),
            )
            return words, scales

        def quantise_w1(b):
            grouped = kept([P, PACK, P, PACK], BF16, f"w1_grouped{b}", "w1_grouped")
            nc.scalar.activation(
                out=grouped[:].rearrange("p t q j -> p q t j"),
                in_=w1_raw[b][:].rearrange("p j (q t) -> p q t j", t=PACK),
                func=ACT.Copy,
            )
            codes = kept([P, BANK], U32, f"w1_codes{b}")
            scales = kept([P, BANK], U8, f"w1_scales{b}")
            nc.vector.quantize_mx(
                out=codes[:].bitcast(FP8X4), scales=scales[:], in_=grouped[:].rearrange("p t q j -> p (t q j)")
            )
            return codes, scales

        w4 = [deal_w4(0)]
        nc.vector.tensor_copy(vw[2][:], tw[2][:].indirect(idx[:]))
        w1q = [quantise_w1(0)]
        for half in range(2):
            nc.vector.tensor_copy(
                vw[1][:, BANK * half : BANK * (half + 1)], tw[1][:].indirect(idx[:, 32 * half : 32 * (half + 1)])
            )
        t2w = {}
        h[0, 0] = load_wish(0, 0)
        w1_raw.append(load_w1(1))
        h[0, 1] = load_wish(0, 1)
        h[0, 2] = load_wish(0, 2)
        h[0, 3] = load_wish(0, 3)
        t2w[0] = load_words(tab2_words[0], T3, "t2w0", "slot0")
        h[1, 0] = load_wish(1, 0)
        h[1, 1] = load_wish(1, 1)
        for q in range(QUADS):
            nc.sync.dma_start(planes2[32 * q : 32 * q + 4, :, :].bitcast(I32), v2s[32 * q : 32 * q + 32 : 4, :].bitcast(I32))
        h[1, 2] = load_wish(1, 2)
        h[1, 3] = load_wish(1, 3)
        t2w[1] = load_words(tab2_words[1], T3, "t2w1", "slot1")


        starts = [sum(CHUNKS[:c]) for c in range(len(CHUNKS))]
        def picked_tiles(name, n, tags):
            return [kept([P, PACK, n], (BF16, F32)[x], f"picked_{name}x{x}", tags[x]) for x in range(2)]

        def pick(picked, start, b, t, x):
            cols = slice(start // 16, (start + picked[x].shape[2]) // 16)
            nc.vector.tensor_copy(picked[x][:, t, :], h[b, t][:].indirect((p1, p2)[x][:, cols]))

        def quantise_picked(picked, name, x):
            n = picked[x].shape[2]
            grouped = ring.tile([P, n, PACK], BF16, name="x_grouped", align_bytes=64, bufs=2)
            regrouped = grouped[:].rearrange("p (c i) t -> p c t i", i=PACK)
            source = picked[x][:].rearrange("p t (c i) -> p c t i", i=PACK)
            if x == 0:
                nc.scalar.copy(regrouped, source)
            else:
                nc.scalar.activation(out=regrouped, in_=source, func=ACT.Abs)
            codes = kept([P, n], U32, f"x_codes{name}{x}")
            scales = kept([P, n], U8, f"x_scales{name}{x}")
            nc.vector.quantize_mx(
                out=codes[:].bitcast(FP8X4), scales=scales[:], in_=grouped[:].rearrange("p n t -> p (n t)")
            )
            return codes, scales

        xq = {}
        w4.append(deal_w4(1))
        w1q.append(quantise_w1(1))
        picked_by_half = {}
        for b in range(2):
            banks = {}
            for t in range(PACK):
                for half in range(2):
                    banks[t, half] = psum.tile([P, BANK], F32, name="bank")

            def stage_one_pass(a, t, half, start, stop):
                cols = slice(BANK * half, BANK * (half + 1))
                if a < 2:
                    weights, weight_scales = w4[b][0][:, a, t, :].bitcast(FP4X4), w4[b][1][:, a, t, :]
                else:
                    rows = slice(P * t, P * (t + 1))
                    weights, weight_scales = w1q[b][0][:, rows].bitcast(FP8X4), w1q[b][1][:, rows]
                nc.tensor.matmul_mx(
                    out=banks[t, half][:], lhsT=weights, lhsT_scale=weight_scales,
                    rhs=vw[a][:, cols].bitcast(FP8X4), rhs_scale=planes[:, a, cols],
                    start=start, stop=stop,
                )

            first, second, final = ((0, 2, 1), (0, 1, 2))[b]
            for a in (first, second):
                for t in range(PACK):
                    for half in range(2):
                        stage_one_pass(a, t, half, a == first, False)
            picked = picked_tiles(f"b{b}", (NP, CHUNKS[0])[b], (("slot2", "picked01"), ("picked10", "picked11"))[b])
            for t in range(PACK):
                squashed = ring.tile([P, S], F32, name="squashed", bufs=3)
                for half in range(2):
                    cols = slice(BANK * half, BANK * (half + 1))
                    stage_one_pass(final, t, half, False, True)
                    nc.scalar.activation(out=squashed[:, cols], in_=banks[t, half][:], func=ACT.Tanh)
                how = HOW[PACK * b + t]
                if how == "V":
                    for cols in (slice(0, BANK), slice(BANK, S)):
                        nc.vector.scalar_tensor_tensor(
                            out=h[b, t][:, cols], in0=squashed[:, cols], scalar=gain_sb[:, b, t : t + 1],
                            in1=h[b, t][:, cols], op0=ALU.mult, op1=ALU.add,
                        )
                else:
                    if how == "S":
                        nc.scalar.activation(out=squashed[:], in_=squashed[:], func=ACT.Copy, scale=gain_sb[:, b, t : t + 1])
                    else:
                        nc.gpsimd.tensor_scalar(
                            out=squashed[:], in0=squashed[:], scalar1=gain_sb[:, b, t : t + 1], scalar2=0.0,
                            op0=ALU.mult, op1=ALU.add,
                        )
                    nc.gpsimd.tensor_tensor(out=h[b, t][:], in0=squashed[:], in1=h[b, t][:], op=ALU.add)
                pick(picked, 0, b, t, 0)
                pick(picked, 0, b, t, 1)
                picked_by_half[b] = picked
                if b == 1 and t == 3:
                    for x in range(2):
                        codes, scales = quantise_picked(picked_by_half[0], "b0", x)
                        for c, n in enumerate(CHUNKS):
                            xq[c, 0, x] = codes[:, starts[c] : starts[c] + n], scales[:, starts[c] : starts[c] + n]
            if b == 1:
                v2w = [kept([P, S2], U32, f"v2w{a}") for a in range(2)]
                for a in range(2):
                    nc.vector.tensor_copy(v2w[a][:], t2w[a][:].indirect(idx2[:]))

        for x in range(2):
            codes, scales = quantise_picked(picked_by_half[1], "b1", x)
            xq[0, 1, x] = codes[:], scales[:]
        out_view = out.rearrange("(m p) n -> p m n", p=P)

        results = {}

        def products(c, x):
            n = CHUNKS[c]
            per_bank = BANK // n
            banks = [psum.tile([P, per_bank, n], F32, name="bank") for k in range(M_TILES // per_bank)]
            for b in range(2):
                for m in range(M_TILES):
                    k, place = divmod(m, per_bank)
                    cols = slice(P * m, P * (m + 1))
                    nc.tensor.matmul_mx(
                        out=banks[k][:, place, :],
                        lhsT=v2w[b][:, cols].bitcast(FP8X4), lhsT_scale=planes2[:, b, cols],
                        rhs=xq[c, b, x][0].bitcast(FP8X4), rhs_scale=xq[c, b, x][1],
                        start=(b == 0 and place == 0), stop=(b == 1 and place == per_bank - 1),
                    )
            return banks

        def best_scores(c):
            n = CHUNKS[c]
            per_bank = BANK // n
            e1, e2 = products(c, 0), products(c, 1)
            results[c] = kept([P, M_TILES, n], F32, f"result{c}")
            for k in range(len(e1)):
                shifted = kept([P, per_bank, n], F32, f"shifted{c}{k}")
                for place in range(per_bank):
                    m = k * per_bank + place
                    nc.scalar.activation(
                        out=shifted[:, place, :], in_=e1[k][:, place, :], func=ACT.Identity,
                        bias=toy_columns[:, 0, m : m + 1],
                    )
                rows = slice(k * per_bank, (k + 1) * per_bank)
                nc.vector.tensor_tensor(out=results[c][:, rows, :], in0=e2[k][:], in1=shifted[:], op=ALU.max)
                weigh(c, rows)

        def weigh(c, rows):
            for m in range(rows.start, rows.stop):
                if c == len(CHUNKS) - 1 and rows.start == 0:
                    nc.scalar.activation(
                        out=results[c][:, m, :], in_=results[c][:, m, :], func=ACT.Copy, scale=toy_columns[:, 1, m : m + 1]
                    )
                elif c == len(CHUNKS) - 1:
                    nc.vector.tensor_scalar(
                        out=results[c][:, m, :], in0=results[c][:, m, :], scalar1=toy_columns[:, 1, m : m + 1],
                        scalar2=None, op0=ALU.mult,
                    )
                else:
                    nc.gpsimd.tensor_scalar(
                        out=results[c][:, m, :], in0=results[c][:, m, :], scalar1=toy_columns[:, 1, m : m + 1],
                        scalar2=0.0, op0=ALU.mult, op1=ALU.add,
                    )
            nc.sync.dma_start(out_view[:, rows, starts[c] : starts[c] + CHUNKS[c]], results[c][:, rows, :])

        def pick_chunk(c, tags):
            picked = picked_tiles(f"c{c}", CHUNKS[c], tags)
            for x in range(2):
                for t in range(PACK):
                    pick(picked, starts[c], 1, t, x)
                codes, scales = quantise_picked(picked, f"c{c}", x)
                xq[c, 1, x] = codes[:], scales[:]

        pick_chunk(1, ("slot1","picked10"))
        best_scores(0)
        best_scores(1)
        pick_chunk(2, ("shifted01","shifted03"))
        best_scores(2)
